import numpy as np
import ml_dtypes


def mxq(x, axis, fmt="e4m3"):
    dtype, down = {"e4m3": (ml_dtypes.float8_e4m3fn, 7), "e5m2": (ml_dtypes.float8_e5m2, 14)}[fmt]
    v = np.moveaxis(np.asarray(x, np.float32).astype(ml_dtypes.bfloat16).astype(np.float64), axis, -1)
    blocks = v.reshape(v.shape[:-1] + (-1, 32))
    amax = np.abs(blocks).max(-1, keepdims=True)
    byte = np.maximum(np.where(amax > 0, np.frexp(amax)[1] - 1 + 127, 0) - down, 1)
    scale = np.exp2(byte - 127.0)
    codes = (blocks / scale).astype(np.float32).astype(dtype).astype(np.float64)
    return np.moveaxis((codes * scale).reshape(v.shape), -1, axis)


WIDE = False


def mx_kscale(k):
    if not WIDE:
        return np.ones(k)
    levels = np.array([10, -10, 5, -5, 0])
    if k % 512:
        return np.exp2(np.random.permutation(np.resize(levels, k // 32))).repeat(32)
    a = np.empty((k // 512, 16))
    for p in range(k // 512):
        a[p, :8] = np.random.permutation(np.resize(levels, 8))
        for g in range(8):
            far = levels[np.abs(levels - a[p, g]) >= 10]
            a[p, g + 8] = far[np.random.randint(len(far))]
    return np.exp2(a.ravel()).repeat(32)


BF16 = ml_dtypes.bfloat16


def bf(x):
    return np.asarray(x, np.float32).astype(BF16)


def f64(x):
    return np.asarray(x).astype(np.float64)


B, N, E, C = 2048, 1024, 512, 512


def metric_distance(q, c, g, h):
    qg = q * g[None, :]
    ch = c * h[None, :]
    cross = mxq(qg, 1, "e4m3") @ mxq(ch, 1, "e4m3").T
    gh = g * h
    q2 = np.sum(gh[None, :] * np.square(q), axis=1)
    c2 = np.sum(gh[None, :] * np.square(c), axis=1)
    return np.sqrt(q2[:, None] + c2[None, :] - 2.0 * cross)


def row_softmax(logit):
    shifted = logit - np.max(logit, axis=1, keepdims=True)
    e = np.exp(shifted)
    return e / np.sum(e, axis=1, keepdims=True)


def draw0():
    s, t = mx_kscale(E), mx_kscale(N)
    return {
        "q": bf(np.random.standard_normal((B, E))),
        "c": bf(np.random.standard_normal((N, E))),
        "g": bf((1.0 + 0.1 * np.random.standard_normal(E)) * s),
        "h": bf((1.0 + 0.1 * np.random.standard_normal(E)) / s),
        "y": bf(np.random.standard_normal((N, C)) / t[:, None]),
        "u": bf(np.random.uniform(size=N)),
        "r": bf(4.0 * np.random.standard_normal(N) * t),
    }


def core(q, c, g, h, y, u, r):
    q, c, g, h, y, u, r = f64(q), f64(c), f64(g), f64(h), f64(y), f64(u), f64(r)
    dist = metric_distance(q, c, g, h)
    keep = u < 0.7
    logit = np.where(keep[None, :], -2.0 * dist, -1e9)
    a = row_softmax(logit)
    ar = a * r[None, :]
    return mxq(ar, 1, "e4m3") @ mxq(y, 0, "e4m3")


def e4m3fn_bytes(y):
    return np.clip(np.asarray(y, np.float64), -448.0, 448.0).astype(np.float32).astype(ml_dtypes.float8_e4m3fn).view(np.uint8)


def e4m3fn_values(b):
    return np.asarray(b, np.uint8).view(ml_dtypes.float8_e4m3fn).astype(np.float64)


def setup_inputs():
    d = draw0()
    x0 = np.asarray(d['y']).astype(np.float64)
    s = (np.max(np.abs(x0), axis=(1,), keepdims=True) / 448.0).astype(np.float32)
    out = {}
    for k, v in d.items():
        if k == 'y':
            out['y_bytes'] = e4m3fn_bytes(x0 / s.astype(np.float64))
            out['y_scale'] = s
        else:
            out[k] = v
    return out


def reference(q, c, g, h, y_bytes, y_scale, u, r):
    return core(q, c, g, h, e4m3fn_values(y_bytes) * y_scale.astype(np.float64), u, r)

@@ -1,0 +1,457 @@
+from contextlib import ExitStack
+
+import concourse.mybir as mybir
+from concourse.masks import make_identity
+
+B, N, E, C = 2048, 1024, 512, 512
+FLOPS = 2 * B * N * E + 2 * B * N * C
+
+F32 = mybir.dt.float32
+BF16 = mybir.dt.bfloat16
+U32 = mybir.dt.uint32
+U8 = mybir.dt.uint8
+F8 = mybir.dt.float8_e4m3fn
+FP8X4 = mybir.dt.float8_e4m3fn_x4
+ALU = mybir.AluOpType
+ACT = mybir.ActivationFunctionType
+
+P = 128
+HALF = 512
+NT = B // P
+NPAIR = NT // 2
+CPAIR = N // P // 2
+FAR = 2.0**58
+KAPPA = 1.5
+QEVEN = False
+G_WEIGH = ()
+
+
+def tile_modernncastochasticneighbourregressor_kernel(tc, q, c, g, h, y_bytes, y_scale, u, r, out):
+    nc = tc.nc
+    with ExitStack() as ctx:
+        keep = ctx.enter_context(tc.tile_pool(name="keep", bufs=1))
+        work = ctx.enter_context(tc.tile_pool(name="work", bufs=2))
+        psum = ctx.enter_context(tc.psum_pool(name="psum", bufs=1))
+
+        ident = keep.tile([P, P], F32, name="ident")
+        ones = keep.tile([P, P], BF16, name="ones")
+        g4 = keep.tile([P, 4], BF16, name="g4")
+        h4 = keep.tile([P, 4], BF16, name="h4")
+        gh4 = keep.tile([P, 4], F32, name="gh4")
+        g_wide = keep.tile([P, 256, 4], BF16, name="g_wide", align_bytes=64)
+        h_wide = keep.tile([P, 256, 4], BF16, name="h_wide", align_bytes=64)
+        u_row = keep.tile([P, N], BF16, name="u_row")
+        far_row = keep.tile([P, N], BF16, name="far_row")
+        r_wide = keep.tile([P, N], BF16, name="r_wide")
+        c2_wide = keep.tile([P, N], F32, name="c2_wide")
+        csq = keep.tile([P, 8, 4, P], F32, name="csq")
+        c_codes = keep.tile([P, N], U32, name="c_codes", align_bytes=64)
+        c_scales = keep.tile([P, N], U8, name="c_scales", align_bytes=64)
+        q_codes = keep.tile([P, B], U32, name="q_codes", align_bytes=64)
+        q_scales = keep.tile([P, B], U8, name="q_scales", align_bytes=64)
+        ghk4 = keep.tile([P, 4], F32, name="ghk4")
+        c2_low = keep.tile([P, 1], F32, name="c2_low")
+        unit = keep.tile([P, NT], F32, name="unit")
+        inv = keep.tile([P, NT], F32, name="inv")
+        q2i = keep.tile([P, NT], F32, name="q2i")
+        two_w = keep.tile([P, NT], F32, name="two_w")
+        neg_w = keep.tile([P, NT], F32, name="neg_w")
+        near = keep.tile([P, NT], F32, name="near")
+        shift = keep.tile([P, NT], F32, name="shift")
+        esum = keep.tile([P, NT], F32, name="esum")
+        rsum = keep.tile([P, NT], F32, name="rsum")
+        dist = keep.tile([P, NT, N], F32, name="dist")
+        yb = keep.tile([P, 2, 4, C], U8, name="yb", align_bytes=64)
+        ysc = keep.tile([P, 2, 4], F32, name="ysc")
+        yw = keep.tile([P, 2, 4, C], BF16, name="yw", align_bytes=64)
+        y_codes = keep.tile([P, 2, C], U32, name="y_codes", align_bytes=64)
+        y_scales = keep.tile([P, 2, C], U8, name="y_scales", align_bytes=64)
+        dummy = keep.tile([P, 1], F32, name="dummy")
+
+        c_v = c.rearrange("(j k p) e -> j p k e", k=2, p=P)
+        q_v = q.rearrange("(j k p) e -> j p k e", k=2, p=P)
+        y_v = y_bytes.rearrange("(g p t) n -> p g t n", p=P, t=4)
+        ysc_v = y_scale.rearrange("(g p t) o -> p g (t o)", p=P, t=4)
+        out_v = out.rearrange("(i p) n -> i p n", p=P)
+
+        ctx.enter_context(tc.manual_schedule())
+
+        rows = {}
+
+        def load_rows(kind, j, view):
+            t = work.tile([P, 2, E], BF16, name="rows", tag="rows", bufs=12)
+            nc.sync.dma_start(out=t[:], in_=view[j])
+            rows[(kind, j)] = t
+
+        nc.scalar.dma_start(out=g4[:], in_=g.rearrange("(p t) -> p t", t=4))
+        nc.scalar.dma_start(out=h4[:], in_=h.rearrange("(p t) -> p t", t=4))
+        nc.scalar.dma_start(out=u_row[0:1, :], in_=u.rearrange("(o n) -> o n", o=1))
+        nc.scalar.dma_start(out=ysc[:], in_=ysc_v)
+        load_rows("c", 0, c_v)
+        load_rows("c", 1, c_v)
+        load_rows("c", 2, c_v)
+        load_rows("c", 3, c_v)
+        for j in range(NPAIR):
+            load_rows("q", j, q_v)
+            if j == 3:
+                nc.sync.dma_start(out=yb[:], in_=y_v)
+        nc.sync.dma_start(out=r_wide[:], in_=r.partition_broadcast(P))
+
+        nc.vector.memset(dummy[:], 1.0)
+        nc.scalar.activation(out=dummy[:], in_=dummy[:], func=ACT.Sqrt)
+        make_identity(nc, ident[:])
+        nc.gpsimd.memset(far_row[:], 0.0)
+        nc.gpsimd.memset(ones[:], 1.0)
+        nc.vector.tensor_copy(out=g_wide[:], in_=g4[:].unsqueeze(1).to_broadcast([P, 256, 4]))
+        nc.vector.tensor_copy(out=h_wide[:], in_=h4[:].unsqueeze(1).to_broadcast([P, 256, 4]))
+        nc.vector.tensor_tensor(out=gh4[:], in0=g4[:], in1=h4[:], op=ALU.mult)
+        nc.vector.tensor_scalar(out=ghk4[:], in0=gh4[:], scalar1=1.0 / KAPPA, scalar2=None, op0=ALU.mult)
+        nc.vector.tensor_scalar(out=far_row[0:1, :], in0=u_row[0:1, :], scalar1=0.7, scalar2=FAR, op0=ALU.is_ge, op1=ALU.mult)
+
+        turned, raws, sqs, prods, q2ps = {}, {}, {}, {}, {}
+
+        def turn(kind, j):
+            if kind == "c":
+                t = psum.tile([P, 4, P], F32, name="bank", tag="bank", bufs=4)
+            else:
+                t = psum.tile([P, 4, P], F32, name="turn", tag="turn", bufs=3)
+            words = rows[(kind, j)][:].bitcast(F32)
+            for k in range(2):
+                for w in range(2):
+                    nc.tensor.transpose(t[:, 2 * k + w, :], words[:, k, w : 256 : 2], ident[:])
+            turned[(kind, j)] = t
+
+        def copy_turn(kind, j):
+            t = turned[(kind, j)]
+            raw = work.tile([P, 2, P, 4], BF16, name="raw", tag="raw", bufs=3, align_bytes=64)
+            mover = nc.vector.tensor_copy if kind == "c" else nc.scalar.copy
+            mover(out=raw[:].bitcast(F32), in_=t[:].rearrange("p (k w) b -> p k b w", k=2))
+            raws[(kind, j)] = raw
+
+        def square_turn(kind, j):
+            t = turned[(kind, j)]
+            if kind == "c":
+                sq = csq[:, 2 * j : 2 * j + 2, :, :]
+            else:
+                sq = work.tile([P, 2, 4, P], F32, name="sq", tag="sq", bufs=3)[:]
+                sqs[j] = sq
+            nc.scalar.activation(
+                out=sq.rearrange("p k t b -> p (k t) b"),
+                in_=t[:].bitcast(BF16).rearrange("p m (b e) -> p m e b", e=2),
+                func=ACT.Square,
+            )
+
+        def weigh(kind, j, eng=None):
+            eng = eng or nc.vector
+            wide = g_wide if kind == "q" else h_wide
+            prod = work.tile([P, 1024], BF16, name="prod", tag="prod", bufs=3, align_bytes=64)
+            eng.tensor_tensor(
+                out=prod[:],
+                in0=raws[(kind, j)][:].rearrange("p k b t -> p (k b t)"),
+                in1=wide[:].rearrange("p b t -> p (b t)"),
+                op=ALU.mult,
+            )
+            prods[(kind, j)] = prod
+
+        def quant(kind, j):
+            codes, scales = (q_codes, q_scales) if kind == "q" else (c_codes, c_scales)
+            cols = slice(256 * j, 256 * j + 256)
+            nc.vector.quantize_mx(out=codes[:, cols].bitcast(FP8X4), scales=scales[:, cols], in_=prods[(kind, j)][:])
+
+        def q2_mm(j):
+            if j % 2 == 0:
+                q2ps[j // 2] = psum.tile([P, 4], F32, name="q2p", tag="q2p", bufs=1)
+            t = q2ps[j // 2]
+            for k in range(2):
+                col = 2 * (j % 2) + k
+                for s in range(4):
+                    nc.tensor.matmul(t[:, col : col + 1], lhsT=sqs[j][:, k, s, :], rhs=ghk4[:, s : s + 1], start=(s == 0), stop=(s == 3))
+
+        def q2_units(m):
+            t = q2ps[m]
+            cols = slice(4 * m, 4 * m + 4)
+            nc.vector.tensor_scalar(out=unit[:, cols], in0=t[:], scalar1=c2_low[:], scalar2=1e-12, op0=ALU.add, op1=ALU.max)
+            nc.vector.reciprocal(out=inv[:, cols], in_=unit[:, cols])
+            nc.vector.scalar_tensor_tensor(out=q2i[:, cols], in0=t[:], scalar=KAPPA, in1=inv[:, cols], op0=ALU.mult, op1=ALU.mult)
+
+        def q2_w(m):
+            cols = slice(4 * m, 4 * m + 4)
+            nc.scalar.activation(out=two_w[:, cols], in_=unit[:, cols], func=ACT.Sqrt, scale=4.0)
+
+        c2ps = {}
+
+        def c2_mm(hf, parts=(0, 1, 2, 3)):
+            cols = slice(HALF * hf, HALF * hf + HALF)
+            if parts[0] == 0:
+                c2_open(hf)
+            t = c2ps[hf]
+            for s in parts:
+                nc.tensor.matmul(
+                    t[:], lhsT=gh4[:, s : s + 1].to_broadcast([P, P]), rhs=csq[:, 4 * hf : 4 * hf + 4, s, :], start=False, stop=(s == 3)
+                )
+
+        def c2_open(hf):
+            tag = "turn" if hf == 0 else "q2p"
+            t = psum.tile([P, HALF], F32, name=tag, tag=tag, bufs=3 if hf == 0 else 1)
+            c2ps[hf] = t
+            cols = slice(HALF * hf, HALF * hf + HALF)
+            nc.tensor.matmul(t[:], lhsT=ones[:], rhs=far_row[:, cols], start=True, stop=False)
+
+        def c2_copy(hf):
+            cols = slice(HALF * hf, HALF * hf + HALF)
+            nc.scalar.copy(out=c2_wide[:, cols], in_=c2ps[hf][:])
+
+        def c2_low_calc():
+            if True:
+                nc.vector.tensor_reduce(out=c2_low[:], in_=c2_wide[:, :P], axis=mybir.AxisListType.X, op=ALU.min)
+                nc.vector.tensor_scalar(out=c2_low[:], in0=c2_low[:], scalar1=1.0 / KAPPA, scalar2=None, op0=ALU.mult)
+
+        crosses, ss = {}, {}
+
+        def cross(i, hfs=(0, 1)):
+            for hf in hfs:
+                t = psum.tile([P, HALF], F32, name="bank", tag="bank", bufs=4)
+                b_cols = slice(P * i, P * i + P)
+                n_cols = slice(HALF * hf, HALF * hf + HALF)
+                nc.tensor.matmul_mx(
+                    out=t[:],
+                    lhsT=q_codes[:, b_cols].bitcast(FP8X4),
+                    lhsT_scale=q_scales[:, b_cols],
+                    rhs=c_codes[:, n_cols].bitcast(FP8X4),
+                    rhs_scale=c_scales[:, n_cols],
+                    start=True,
+                    stop=True,
+                )
+                crosses[(i, hf)] = t
+
+        def add_c2(i, hfs=(0, 1)):
+            s = dist[:, i, :]
+            for hf in hfs:
+                n_cols = slice(HALF * hf, HALF * hf + HALF)
+                nc.vector.scalar_tensor_tensor(
+                    out=s[:, n_cols], in0=crosses[(i, hf)][:], scalar=-2.0, in1=c2_wide[:, n_cols], op0=ALU.mult, op1=ALU.add
+                )
+            ss[i] = s
+
+        lows = {}
+
+        def narrow(i):
+            low = work.tile([P, N], BF16, name="low", tag="low", bufs=3)
+            nc.gpsimd.tensor_scalar(out=low[:], in0=dist[:, i, :], scalar1=1.0, scalar2=0.0, op0=ALU.mult, op1=ALU.add)
+            lows[i] = low
+
+        def row_min(i):
+            junk = work.tile([P, N], BF16, name="junk", tag="junk", bufs=1)
+            nc.vector.tensor_scalar(
+                out=junk[:], in0=lows[i][:], scalar1=1.0, scalar2=None, op0=ALU.mult, op1=ALU.min, accum_out=near[:, i : i + 1]
+            )
+
+        def root(i):
+            nc.scalar.activation(out=dist[:, i, :], in_=ss[i], func=ACT.Sqrt, bias=q2i[:, i : i + 1], scale=inv[:, i : i + 1])
+
+        def shifts(i0, i1):
+            cols = slice(i0, i1)
+            nc.vector.tensor_scalar(out=neg_w[:, cols], in0=two_w[:, cols], scalar1=-1.0, scalar2=None, op0=ALU.mult)
+            nc.vector.tensor_tensor(out=shift[:, cols], in0=two_w[:, cols], in1=near[:, cols], op=ALU.mult)
+
+        def y_widen(k):
+            gg, t = k // 4, k % 4
+            nc.scalar.activation(out=yw[:, gg, t, :], in_=yb[:, gg, t, :].bitcast(F8), func=ACT.Copy, scale=ysc[:, gg, t : t + 1])
+
+        yis = {}
+
+        def y_mix(gg):
+            yi = work.tile([P, C, 4], BF16, name="yi", tag="yi", bufs=2, align_bytes=64)
+            nc.vector.tensor_copy(out=yi[:], in_=yw[:, gg, :, :].rearrange("p t n -> p n t"))
+            yis[gg] = yi
+
+        def y_quant(gg):
+            nc.vector.quantize_mx(
+                out=y_codes[:, gg, :].bitcast(FP8X4), scales=y_scales[:, gg, :], in_=yis[gg][:].rearrange("p n t -> p (n t)")
+            )
+
+        for j in range(4):
+            turn("c", j)
+            square_turn("c", j)
+            if j == 3:
+                turn("q", 0)
+            if j == 1:
+                copy_turn("c", 0)
+                copy_turn("c", 1)
+                weigh("c", 0)
+                weigh("c", 1)
+        c2_mm(0)
+        copy_turn("q", 0)
+        copy_turn("c", 2)
+        quant("c", 0)
+        copy_turn("c", 3)
+        weigh("c", 2)
+        quant("c", 1)
+        weigh("c", 3)
+        weigh("q", 0)
+        square_turn("q", 0)
+        quant("c", 2)
+        quant("c", 3)
+        quant("q", 0)
+        turn("q", 1)
+        c2_copy(0)
+        copy_turn("q", 1)
+        c2_mm(1, (0,))
+        cross(0, (0,))
+        add_c2(0, (0,))
+        turn("q", 2)
+        copy_turn("q", 2)
+        c2_mm(1, (1,))
+        cross(1, (0,))
+        weigh("q", 1)
+        add_c2(1, (0,))
+        quant("q", 1)
+        square_turn("q", 1)
+        c2_mm(1, (2,))
+        c2_low_calc()
+        cross(2, (0,))
+        cross(3, (0,))
+        add_c2(2, (0,))
+        weigh("q", 2)
+        add_c2(3, (0,))
+        c2_mm(1, (3,))
+        quant("q", 2)
+        cross(4, (0,))
+        c2_copy(1)
+        square_turn("q", 2)
+        q2_mm(0)
+        cross(5, (0,))
+        add_c2(4, (0,))
+        cross(0, (1,))
+        q2_mm(1)
+        add_c2(5, (0,))
+        turn("q", 3)
+        q2_units(0)
+        cross(1, (1,))
+        add_c2(0, (1,))
+        copy_turn("q", 3)
+        cross(2, (1,))
+        add_c2(1, (1,))
+        for i in range(NT):
+            even, j = i % 2 == 0, i // 2
+            live = lambda p: 3 <= p < NPAIR
+            if i + 3 < 6:
+                cross(i + 3, (1,))
+            elif i + 3 < NT:
+                cross(i + 3)
+            if even and live(j + 4):
+                turn("q", j + 4)
+            if even and live(j + 3) and (j + 3) in G_WEIGH:
+                weigh("q", j + 3, nc.gpsimd)
+            root(i)
+            narrow(i)
+            if i + 2 < 6:
+                add_c2(i + 2, (1,))
+            elif i + 2 < NT:
+                add_c2(i + 2)
+            if even and live(j + 3):
+                if (j + 3) not in G_WEIGH:
+                    weigh("q", j + 3)
+                square_turn("q", j + 3)
+            if i > 0:
+                row_min(i - 1)
+            if i % 4 == 2 and i + 2 < NT:
+                q2_units((i + 2) // 4)
+            if not even and live(j + 4):
+                copy_turn("q", j + 4)
+            if QEVEN and even and live(j + 3):
+                quant("q", j + 3)
+            if not QEVEN and not even and live(j + 3):
+                quant("q", j + 3)
+            if i == 0:
+                q2_mm(2)
+            if not even and live(j + 3):
+                q2_mm(j + 3)
+            if i % 4 == 0:
+                q2_w(i // 4)
+            if i == 9:
+                shifts(0, 8)
+            if 4 <= i < 12:
+                y_widen(i - 4)
+        y_mix(0)
+        row_min(NT - 1)
+        shifts(8, 16)
+        y_quant(0)
+        y_mix(1)
+        y_quant(1)
+
+        es, ars, ats, gs, acs, ass, os_ = {}, {}, {}, {}, {}, {}, {}
+
+        def expo(i):
+            e = work.tile([P, N], F32, name="e", tag="e", bufs=3)
+            nc.scalar.activation(
+                out=e[:], in_=dist[:, i, :], func=ACT.Exp, bias=shift[:, i : i + 1], scale=neg_w[:, i : i + 1], accum_out=esum[:, i : i + 1]
+            )
+            es[i] = e
+
+        def scale_ar(i):
+            nc.vector.reciprocal(out=rsum[:, i : i + 1], in_=esum[:, i : i + 1])
+            ar = work.tile([P, N], BF16, name="ar", tag="ar", bufs=3, align_bytes=64)
+            nc.vector.scalar_tensor_tensor(
+                out=ar[:], in0=es[i][:], scalar=rsum[:, i : i + 1], in1=r_wide[:], op0=ALU.mult, op1=ALU.mult
+            )
+            ars[i] = ar
+
+        def turn_ar(i):
+            t = psum.tile([P, 4, P], F32, name="turn", tag="turn", bufs=3)
+            words = ars[i][:].bitcast(F32)
+            for gg in range(2):
+                for w in range(2):
+                    nc.tensor.transpose(t[:, 2 * gg + w, :], words[:, 256 * gg + w : 256 * gg + 256 : 2], ident[:])
+            ats[i] = t
+
+        def empty_ar(i):
+            a_in = work.tile([P, 2, P, 4], BF16, name="a_in", tag="a_in", bufs=3, align_bytes=64)
+            nc.scalar.copy(out=a_in[:].bitcast(F32), in_=ats[i][:].rearrange("p (k w) b -> p k b w", k=2))
+            gs[i] = a_in
+
+        def quant_ar(i):
+            codes = work.tile([P, 2, P], U32, name="a_codes", tag="a_codes", bufs=3, align_bytes=64)
+            scales = work.tile([P, 2, P], U8, name="a_scales", tag="a_scales", bufs=3, align_bytes=64)
+            nc.vector.quantize_mx(
+                out=codes[:].rearrange("p g b -> p (g b)").bitcast(FP8X4),
+                scales=scales[:].rearrange("p g b -> p (g b)"),
+                in_=gs[i][:].rearrange("p k b t -> p (k b t)"),
+            )
+            acs[i], ass[i] = codes, scales
+
+        def mm_out(i):
+            t = psum.tile([P, HALF], F32, name="bank", tag="bank", bufs=4)
+            for gg in range(2):
+                nc.tensor.matmul_mx(
+                    out=t[:],
+                    lhsT=acs[i][:, gg, :].bitcast(FP8X4),
+                    lhsT_scale=ass[i][:, gg, :],
+                    rhs=y_codes[:, gg, :].bitcast(FP8X4),
+                    rhs_scale=y_scales[:, gg, :],
+                    start=(gg == 0),
+                    stop=(gg == 1),
+                )
+            os_[i] = t
+
+        def store(i):
+            o = work.tile([P, C], F32, name="o", tag="o", bufs=3)
+            if i % 2 == 1:
+                nc.scalar.copy(out=o[:], in_=os_[i][:])
+            else:
+                nc.vector.tensor_copy(out=o[:], in_=os_[i][:])
+            nc.sync.dma_start(out=out_v[i], in_=o[:])
+
+        for k in range(NT + 4):
+            if k < NT:
+                expo(k)
+            if 0 <= k - 1 < NT:
+                scale_ar(k - 1)
+                turn_ar(k - 1)
+            if 0 <= k - 2 < NT:
+                empty_ar(k - 2)
+            if 0 <= k - 3 < NT:
+                quant_ar(k - 3)
+                mm_out(k - 3)
+            if 0 <= k - 4 < NT:
+                store(k - 4)

@@ -22,8 +22,7 @@ NPAIR = NT // 2
 CPAIR = N // P // 2
 FAR = 2.0**58
 KAPPA = 1.5
-QEVEN = False
-G_WEIGH = ()
+MIN_LATE = 13
 
 
 def tile_modernncastochasticneighbourregressor_kernel(tc, q, c, g, h, y_bytes, y_scale, u, r, out):
@@ -44,7 +43,7 @@ def tile_modernncastochasticneighbourregressor_kernel(tc, q, c, g, h, y_bytes, y
         far_row = keep.tile([P, N], BF16, name="far_row")
         r_wide = keep.tile([P, N], BF16, name="r_wide")
         c2_wide = keep.tile([P, N], F32, name="c2_wide")
-        csq = keep.tile([P, 8, 4, P], F32, name="csq")
+        csq = keep.tile([P, 4, N], F32, name="csq")
         c_codes = keep.tile([P, N], U32, name="c_codes", align_bytes=64)
         c_scales = keep.tile([P, N], U8, name="c_scales", align_bytes=64)
         q_codes = keep.tile([P, B], U32, name="q_codes", align_bytes=64)
@@ -91,10 +90,11 @@ def tile_modernncastochasticneighbourregressor_kernel(tc, q, c, g, h, y_bytes, y
         load_rows("c", 1, c_v)
         load_rows("c", 2, c_v)
         load_rows("c", 3, c_v)
-        for j in range(NPAIR):
+        load_rows("q", 0, q_v)
+        load_rows("q", 1, q_v)
+        nc.sync.dma_start(out=yb[:], in_=y_v)
+        for j in range(2, NPAIR):
             load_rows("q", j, q_v)
-            if j == 3:
-                nc.sync.dma_start(out=yb[:], in_=y_v)
         nc.sync.dma_start(out=r_wide[:], in_=r.partition_broadcast(P))
 
         nc.vector.memset(dummy[:], 1.0)
@@ -108,47 +108,38 @@ def tile_modernncastochasticneighbourregressor_kernel(tc, q, c, g, h, y_bytes, y
         nc.vector.tensor_scalar(out=ghk4[:], in0=gh4[:], scalar1=1.0 / KAPPA, scalar2=None, op0=ALU.mult)
         nc.vector.tensor_scalar(out=far_row[0:1, :], in0=u_row[0:1, :], scalar1=0.7, scalar2=FAR, op0=ALU.is_ge, op1=ALU.mult)
 
-        turned, raws, sqs, prods, q2ps = {}, {}, {}, {}, {}
+        turned, sqs, prods, q2ps = {}, {}, {}, {}
 
         def turn(kind, j):
             if kind == "c":
-                t = psum.tile([P, 4, P], F32, name="bank", tag="bank", bufs=4)
+                t = psum.tile([P, 2, 2, P], F32, name="bank", tag="bank", bufs=4)
             else:
-                t = psum.tile([P, 4, P], F32, name="turn", tag="turn", bufs=3)
+                t = psum.tile([P, 2, 2, P], F32, name="turn", tag="turn", bufs=3)
             words = rows[(kind, j)][:].bitcast(F32)
             for k in range(2):
                 for w in range(2):
-                    nc.tensor.transpose(t[:, 2 * k + w, :], words[:, k, w : 256 : 2], ident[:])
-            turned[(kind, j)] = t
-
-        def copy_turn(kind, j):
-            t = turned[(kind, j)]
-            raw = work.tile([P, 2, P, 4], BF16, name="raw", tag="raw", bufs=3, align_bytes=64)
-            mover = nc.vector.tensor_copy if kind == "c" else nc.scalar.copy
-            mover(out=raw[:].bitcast(F32), in_=t[:].rearrange("p (k w) b -> p k b w", k=2))
-            raws[(kind, j)] = raw
+                    nc.tensor.transpose(t[:, w, k, :], words[:, k, w : 256 : 2], ident[:])
+            turned[(kind, j)] = t[:].rearrange("p w k b -> p w (k b)").bitcast(BF16).rearrange("p w (b e) -> p w b e", e=2)
 
         def square_turn(kind, j):
-            t = turned[(kind, j)]
             if kind == "c":
-                sq = csq[:, 2 * j : 2 * j + 2, :, :]
+                sq = csq[:, :, 256 * j : 256 * j + 256]
             else:
-                sq = work.tile([P, 2, 4, P], F32, name="sq", tag="sq", bufs=3)[:]
-                sqs[j] = sq
+                sqs[j] = work.tile([P, 4, 256], F32, name="sq", tag="sq", bufs=3)
+                sq = sqs[j][:]
             nc.scalar.activation(
-                out=sq.rearrange("p k t b -> p (k t) b"),
-                in_=t[:].bitcast(BF16).rearrange("p m (b e) -> p m e b", e=2),
+                out=sq.rearrange("p (w e) b -> p w e b", e=2),
+                in_=turned[(kind, j)].rearrange("p w b e -> p w e b"),
                 func=ACT.Square,
             )
 
-        def weigh(kind, j, eng=None):
-            eng = eng or nc.vector
+        def weigh(kind, j):
             wide = g_wide if kind == "q" else h_wide
             prod = work.tile([P, 1024], BF16, name="prod", tag="prod", bufs=3, align_bytes=64)
-            eng.tensor_tensor(
-                out=prod[:],
-                in0=raws[(kind, j)][:].rearrange("p k b t -> p (k b t)"),
-                in1=wide[:].rearrange("p b t -> p (b t)"),
+            nc.vector.tensor_tensor(
+                out=prod[:].rearrange("p (b w e) -> p b w e", w=2, e=2),
+                in0=turned[(kind, j)].rearrange("p w b e -> p b w e"),
+                in1=wide[:].rearrange("p b (w e) -> p b w e", e=2),
                 op=ALU.mult,
             )
             prods[(kind, j)] = prod
@@ -165,7 +156,7 @@ def tile_modernncastochasticneighbourregressor_kernel(tc, q, c, g, h, y_bytes, y
             for k in range(2):
                 col = 2 * (j % 2) + k
                 for s in range(4):
-                    nc.tensor.matmul(t[:, col : col + 1], lhsT=sqs[j][:, k, s, :], rhs=ghk4[:, s : s + 1], start=(s == 0), stop=(s == 3))
+                    nc.tensor.matmul(t[:, col : col + 1], lhsT=sqs[j][:, s, P * k : P * k + P], rhs=ghk4[:, s : s + 1], start=(s == 0), stop=(s == 3))
 
         def q2_units(m):
             t = q2ps[m]
@@ -187,12 +178,11 @@ def tile_modernncastochasticneighbourregressor_kernel(tc, q, c, g, h, y_bytes, y
             t = c2ps[hf]
             for s in parts:
                 nc.tensor.matmul(
-                    t[:], lhsT=gh4[:, s : s + 1].to_broadcast([P, P]), rhs=csq[:, 4 * hf : 4 * hf + 4, s, :], start=False, stop=(s == 3)
+                    t[:], lhsT=gh4[:, s : s + 1].to_broadcast([P, P]), rhs=csq[:, s, cols], start=False, stop=(s == 3)
                 )
 
         def c2_open(hf):
-            tag = "turn" if hf == 0 else "q2p"
-            t = psum.tile([P, HALF], F32, name=tag, tag=tag, bufs=3 if hf == 0 else 1)
+            t = psum.tile([P, HALF], F32, name="turn", tag="turn", bufs=3)
             c2ps[hf] = t
             cols = slice(HALF * hf, HALF * hf + HALF)
             nc.tensor.matmul(t[:], lhsT=ones[:], rhs=far_row[:, cols], start=True, stop=False)
@@ -262,7 +252,9 @@ def tile_modernncastochasticneighbourregressor_kernel(tc, q, c, g, h, y_bytes, y
 
         def y_mix(gg):
             yi = work.tile([P, C, 4], BF16, name="yi", tag="yi", bufs=2, align_bytes=64)
-            nc.vector.tensor_copy(out=yi[:], in_=yw[:, gg, :, :].rearrange("p t n -> p n t"))
+            nc.gpsimd.tensor_scalar(
+                out=yi[:], in0=yw[:, gg, :, :].rearrange("p t n -> p n t"), scalar1=1.0, scalar2=0.0, op0=ALU.mult, op1=ALU.add
+            )
             yis[gg] = yi
 
         def y_quant(gg):
@@ -273,114 +265,109 @@ def tile_modernncastochasticneighbourregressor_kernel(tc, q, c, g, h, y_bytes, y
         for j in range(4):
             turn("c", j)
             square_turn("c", j)
-            if j == 3:
-                turn("q", 0)
-            if j == 1:
-                copy_turn("c", 0)
-                copy_turn("c", 1)
-                weigh("c", 0)
-                weigh("c", 1)
-        c2_mm(0)
-        copy_turn("q", 0)
-        copy_turn("c", 2)
-        quant("c", 0)
-        copy_turn("c", 3)
-        weigh("c", 2)
-        quant("c", 1)
-        weigh("c", 3)
-        weigh("q", 0)
-        square_turn("q", 0)
-        quant("c", 2)
-        quant("c", 3)
-        quant("q", 0)
+            weigh("c", j)
+            if j > 1:
+                quant("c", j - 2)
+        turn("q", 0)
         turn("q", 1)
-        c2_copy(0)
-        copy_turn("q", 1)
-        c2_mm(1, (0,))
-        cross(0, (0,))
-        add_c2(0, (0,))
-        turn("q", 2)
-        copy_turn("q", 2)
-        c2_mm(1, (1,))
-        cross(1, (0,))
+        c2_mm(0)
+        weigh("q", 0)
+        quant("c", 2)
         weigh("q", 1)
-        add_c2(1, (0,))
+        quant("c", 3)
+        square_turn("q", 0)
+        quant("q", 0)
+        y_widen(0)
         quant("q", 1)
+        cross(0, (0,))
+        cross(1, (0,))
+        c2_copy(0)
         square_turn("q", 1)
+        turn("q", 2)
+        cross(2, (0,))
+        c2_mm(1, (0,))
+        cross(3, (0,))
+        y_widen(1)
+        add_c2(0, (0,))
+        add_c2(1, (0,))
+        weigh("q", 2)
+        square_turn("q", 2)
+        add_c2(2, (0,))
+        turn("q", 3)
+        quant("q", 2)
+        add_c2(3, (0,))
+        c2_mm(1, (1,))
+        cross(4, (0,))
+        y_widen(2)
+        y_widen(3)
+        y_mix(0)
         c2_mm(1, (2,))
         c2_low_calc()
-        cross(2, (0,))
-        cross(3, (0,))
-        add_c2(2, (0,))
-        weigh("q", 2)
-        add_c2(3, (0,))
-        c2_mm(1, (3,))
-        quant("q", 2)
-        cross(4, (0,))
-        c2_copy(1)
-        square_turn("q", 2)
-        q2_mm(0)
         cross(5, (0,))
+        weigh("q", 3)
         add_c2(4, (0,))
+        q2_mm(0)
+        quant("q", 3)
+        add_c2(5, (0,))
+        c2_mm(1, (3,))
+        cross(6, (0,))
+        add_c2(6, (0,))
+        c2_copy(1)
         cross(0, (1,))
         q2_mm(1)
-        add_c2(5, (0,))
-        turn("q", 3)
-        q2_units(0)
         cross(1, (1,))
+        cross(7, (0,))
         add_c2(0, (1,))
-        copy_turn("q", 3)
+        y_widen(4)
+        q2_units(0)
+        square_turn("q", 3)
+        add_c2(7, (0,))
         cross(2, (1,))
         add_c2(1, (1,))
         for i in range(NT):
             even, j = i % 2 == 0, i // 2
-            live = lambda p: 3 <= p < NPAIR
-            if i + 3 < 6:
+            live = lambda p: 4 <= p < NPAIR
+            if i + 3 < 8:
                 cross(i + 3, (1,))
             elif i + 3 < NT:
                 cross(i + 3)
             if even and live(j + 4):
                 turn("q", j + 4)
-            if even and live(j + 3) and (j + 3) in G_WEIGH:
-                weigh("q", j + 3, nc.gpsimd)
             root(i)
             narrow(i)
-            if i + 2 < 6:
+            if i + 2 < 8:
                 add_c2(i + 2, (1,))
             elif i + 2 < NT:
                 add_c2(i + 2)
-            if even and live(j + 3):
-                if (j + 3) not in G_WEIGH:
-                    weigh("q", j + 3)
-                square_turn("q", j + 3)
-            if i > 0:
-                row_min(i - 1)
-            if i % 4 == 2 and i + 2 < NT:
-                q2_units((i + 2) // 4)
             if not even and live(j + 4):
-                copy_turn("q", j + 4)
-            if QEVEN and even and live(j + 3):
-                quant("q", j + 3)
-            if not QEVEN and not even and live(j + 3):
+                weigh("q", j + 4)
+                square_turn("q", j + 4)
+            if 0 <= i - 2 < MIN_LATE:
+                row_min(i - 2)
+            if i % 4 == 1 and i + 3 < NT:
+                q2_units((i + 3) // 4)
+            if even and live(j + 3):
                 quant("q", j + 3)
             if i == 0:
                 q2_mm(2)
-            if not even and live(j + 3):
+                q2_mm(3)
+            if even and live(j + 3):
                 q2_mm(j + 3)
             if i % 4 == 0:
                 q2_w(i // 4)
-            if i == 9:
+            if i < 3:
+                y_widen(i + 5)
+            if i == 4:
+                y_mix(1)
+            if i == 11:
                 shifts(0, 8)
-            if 4 <= i < 12:
-                y_widen(i - 4)
-        y_mix(0)
-        row_min(NT - 1)
-        shifts(8, 16)
+        for i in range(MIN_LATE, NT):
+            row_min(i)
         y_quant(0)
-        y_mix(1)
         y_quant(1)
+        shifts(8, 16)
 
-        es, ars, ats, gs, acs, ass, os_ = {}, {}, {}, {}, {}, {}, {}
+        es, ars, ats, ins, acs, os_ = {}, {}, {}, {}, {}, {}
 
         def expo(i):
             e = work.tile([P, N], F32, name="e", tag="e", bufs=3)
@@ -389,69 +376,98 @@ def tile_modernncastochasticneighbourregressor_kernel(tc, q, c, g, h, y_bytes, y
             )
             es[i] = e
 
-        def scale_ar(i):
+        def invert(i):
             nc.vector.reciprocal(out=rsum[:, i : i + 1], in_=esum[:, i : i + 1])
-            ar = work.tile([P, N], BF16, name="ar", tag="ar", bufs=3, align_bytes=64)
+
+        def scale_ar(i, gs=(0, 1)):
+            cols = slice(512 * gs[0], 512 * gs[-1] + 512)
+            ar = work.tile([P, 512 * len(gs)], BF16, name="ar", tag="ar", bufs=3, align_bytes=64)
             nc.vector.scalar_tensor_tensor(
-                out=ar[:], in0=es[i][:], scalar=rsum[:, i : i + 1], in1=r_wide[:], op0=ALU.mult, op1=ALU.mult
+                out=ar[:], in0=es[i][:, cols], scalar=rsum[:, i : i + 1], in1=r_wide[:, cols], op0=ALU.mult, op1=ALU.mult
             )
-            ars[i] = ar
+            ars[(i, gs)] = ar
 
-        def turn_ar(i):
-            t = psum.tile([P, 4, P], F32, name="turn", tag="turn", bufs=3)
-            words = ars[i][:].bitcast(F32)
-            for gg in range(2):
+        def turn_ar(i, gs=(0, 1)):
+            t = psum.tile([P, len(gs), 2, P], F32, name="turn", tag="turn", bufs=3)
+            words = ars[(i, gs)][:].bitcast(F32)
+            for gg in range(len(gs)):
                 for w in range(2):
-                    nc.tensor.transpose(t[:, 2 * gg + w, :], words[:, 256 * gg + w : 256 * gg + 256 : 2], ident[:])
-            ats[i] = t
+                    nc.tensor.transpose(t[:, gg, w, :], words[:, 256 * gg + w : 256 * gg + 256 : 2], ident[:])
+            ats[(i, gs)] = t
 
-        def empty_ar(i):
-            a_in = work.tile([P, 2, P, 4], BF16, name="a_in", tag="a_in", bufs=3, align_bytes=64)
-            nc.scalar.copy(out=a_in[:].bitcast(F32), in_=ats[i][:].rearrange("p (k w) b -> p k b w", k=2))
-            gs[i] = a_in
+        def empty_ar(i, gs=(0, 1), mover=None):
+            mover = mover or nc.scalar.copy
+            a_in = work.tile([P, len(gs), P, 4], BF16, name="a_in", tag="a_in", bufs=3, align_bytes=64)
+            mover(out=a_in[:].bitcast(F32), in_=ats[(i, gs)][:].rearrange("p g w b -> p g b w"))
+            ins[(i, gs)] = a_in
 
-        def quant_ar(i):
-            codes = work.tile([P, 2, P], U32, name="a_codes", tag="a_codes", bufs=3, align_bytes=64)
-            scales = work.tile([P, 2, P], U8, name="a_scales", tag="a_scales", bufs=3, align_bytes=64)
+        def quant_ar(i, gs=(0, 1)):
+            codes = work.tile([P, len(gs), P], U32, name="a_codes", tag="a_codes", bufs=3, align_bytes=64)
+            scales = work.tile([P, len(gs), P], U8, name="a_scales", tag="a_scales", bufs=3, align_bytes=64)
             nc.vector.quantize_mx(
                 out=codes[:].rearrange("p g b -> p (g b)").bitcast(FP8X4),
                 scales=scales[:].rearrange("p g b -> p (g b)"),
-                in_=gs[i][:].rearrange("p k b t -> p (k b t)"),
+                in_=ins[(i, gs)][:].rearrange("p g b t -> p (g b t)"),
             )
-            acs[i], ass[i] = codes, scales
+            for n, gg in enumerate(gs):
+                acs[(i, gg)] = codes[:, n, :], scales[:, n, :]
 
-        def mm_out(i):
-            t = psum.tile([P, HALF], F32, name="bank", tag="bank", bufs=4)
-            for gg in range(2):
+        def mm_out(i, gs=(0, 1)):
+            if gs[0] == 0:
+                os_[i] = psum.tile([P, HALF], F32, name="bank", tag="bank", bufs=4)
+            for gg in gs:
+                codes, scales = acs[(i, gg)]
                 nc.tensor.matmul_mx(
-                    out=t[:],
-                    lhsT=acs[i][:, gg, :].bitcast(FP8X4),
-                    lhsT_scale=ass[i][:, gg, :],
+                    out=os_[i][:],
+                    lhsT=codes.bitcast(FP8X4),
+                    lhsT_scale=scales,
                     rhs=y_codes[:, gg, :].bitcast(FP8X4),
                     rhs_scale=y_scales[:, gg, :],
                     start=(gg == 0),
                     stop=(gg == 1),
                 )
-            os_[i] = t
 
         def store(i):
-            o = work.tile([P, C], F32, name="o", tag="o", bufs=3)
+            o = work.tile([P, C], F32, name="o", tag="o", bufs=5)
             if i % 2 == 1:
                 nc.scalar.copy(out=o[:], in_=os_[i][:])
             else:
                 nc.vector.tensor_copy(out=o[:], in_=os_[i][:])
             nc.sync.dma_start(out=out_v[i], in_=o[:])
 
-        for k in range(NT + 4):
+        def store_halves(i):
+            for cc, mover in ((0, nc.scalar.copy), (1, nc.vector.tensor_copy)):
+                o = work.tile([P, C // 2], F32, name="o", tag="o", bufs=5)
+                cols = slice(256 * cc, 256 * cc + 256)
+                mover(out=o[:], in_=os_[i][:, cols])
+                nc.sync.dma_start(out=out_v[i][:, cols], in_=o[:])
+
+        last = NT - 1
+        for k in range(NT + 2):
             if k < NT:
                 expo(k)
-            if 0 <= k - 1 < NT:
+            if 0 <= k - 1 < last:
                 scale_ar(k - 1)
                 turn_ar(k - 1)
-            if 0 <= k - 2 < NT:
+            if k - 1 == last:
+                scale_ar(last, (0,))
+                turn_ar(last, (0,))
+                scale_ar(last, (1,))
+                turn_ar(last, (1,))
+            if 0 <= k - 2 < last:
                 empty_ar(k - 2)
-            if 0 <= k - 3 < NT:
+            if 0 <= k - 3 < last:
                 quant_ar(k - 3)
                 mm_out(k - 3)
-            if 0 <= k - 4 < NT:
+            if k < NT:
+                invert(k)
+            if 0 <= k - 4 < last:
                 store(k - 4)
+        empty_ar(last, (0,))
+        quant_ar(last, (0,))
+        mm_out(last, (0,))
+        empty_ar(last, (1,), nc.vector.tensor_copy)
+        quant_ar(last, (1,))
+        mm_out(last, (1,))
+        store(last - 1)
+        store_halves(last)

@@ -34,6 +34,7 @@ def tile_modernncastochasticneighbourregressor_kernel(tc, q, c, g, h, y_bytes, y
 
         ident = keep.tile([P, P], F32, name="ident")
         ones = keep.tile([P, P], BF16, name="ones")
+        sorter = keep.tile([P, P], F32, name="sorter")
         g4 = keep.tile([P, 4], BF16, name="g4")
         h4 = keep.tile([P, 4], BF16, name="h4")
         gh4 = keep.tile([P, 4], F32, name="gh4")
@@ -41,9 +42,10 @@ def tile_modernncastochasticneighbourregressor_kernel(tc, q, c, g, h, y_bytes, y
         h_wide = keep.tile([P, 256, 4], BF16, name="h_wide", align_bytes=64)
         u_row = keep.tile([P, N], BF16, name="u_row")
         far_row = keep.tile([P, N], BF16, name="far_row")
+        r_raw = keep.tile([P, N], BF16, name="r_raw")
         r_wide = keep.tile([P, N], BF16, name="r_wide")
         c2_wide = keep.tile([P, N], F32, name="c2_wide")
-        csq = keep.tile([P, 4, N], F32, name="csq")
+        csq = keep.tile([P, 4, 2, 2, 2, P], F32, name="csq")
         c_codes = keep.tile([P, N], U32, name="c_codes", align_bytes=64)
         c_scales = keep.tile([P, N], U8, name="c_scales", align_bytes=64)
         q_codes = keep.tile([P, B], U32, name="q_codes", align_bytes=64)
@@ -95,43 +97,63 @@ def tile_modernncastochasticneighbourregressor_kernel(tc, q, c, g, h, y_bytes, y
         nc.sync.dma_start(out=yb[:], in_=y_v)
         for j in range(2, NPAIR):
             load_rows("q", j, q_v)
-        nc.sync.dma_start(out=r_wide[:], in_=r.partition_broadcast(P))
+        nc.sync.dma_start(out=r_raw[:], in_=r.partition_broadcast(P))
 
         nc.vector.memset(dummy[:], 1.0)
         nc.scalar.activation(out=dummy[:], in_=dummy[:], func=ACT.Sqrt)
         make_identity(nc, ident[:])
+        nc.vector.tensor_copy(
+            out=sorter[:].rearrange("p (v x e) -> p v x e", v=2, e=2), in_=ident[:].rearrange("p (x v e) -> p v x e", v=2, e=2)
+        )
         nc.gpsimd.memset(far_row[:], 0.0)
         nc.gpsimd.memset(ones[:], 1.0)
         nc.vector.tensor_copy(out=g_wide[:], in_=g4[:].unsqueeze(1).to_broadcast([P, 256, 4]))
         nc.vector.tensor_copy(out=h_wide[:], in_=h4[:].unsqueeze(1).to_broadcast([P, 256, 4]))
         nc.vector.tensor_tensor(out=gh4[:], in0=g4[:], in1=h4[:], op=ALU.mult)
         nc.vector.tensor_scalar(out=ghk4[:], in0=gh4[:], scalar1=1.0 / KAPPA, scalar2=None, op0=ALU.mult)
-        nc.vector.tensor_scalar(out=far_row[0:1, :], in0=u_row[0:1, :], scalar1=0.7, scalar2=FAR, op0=ALU.is_ge, op1=ALU.mult)
+        for gg in range(2):
+            cols = slice(512 * gg, 512 * gg + 512)
+            nc.vector.tensor_scalar(
+                out=far_row[0:1, cols].rearrange("o (v x e) -> o v x e", v=2, e=2),
+                in0=u_row[0:1, cols].rearrange("o (x v e) -> o v x e", v=2, e=2),
+                scalar1=0.7,
+                scalar2=FAR,
+                op0=ALU.is_ge,
+                op1=ALU.mult,
+            )
 
         turned, sqs, prods, q2ps = {}, {}, {}, {}
 
         def turn(kind, j):
+            words = rows[(kind, j)][:].bitcast(F32)
             if kind == "c":
-                t = psum.tile([P, 2, 2, P], F32, name="bank", tag="bank", bufs=4)
+                t = psum.tile([P, 2, 2, 2, P // 2], F32, name="bank", tag="bank", bufs=4)
+                for k in range(2):
+                    for w in range(2):
+                        nc.tensor.transpose(t[:, w, :, k, :], words[:, k, w : 256 : 2], sorter[:])
+                flat = t[:].rearrange("p w v k y -> p w (v k y)")
             else:
                 t = psum.tile([P, 2, 2, P], F32, name="turn", tag="turn", bufs=3)
-            words = rows[(kind, j)][:].bitcast(F32)
-            for k in range(2):
-                for w in range(2):
-                    nc.tensor.transpose(t[:, w, k, :], words[:, k, w : 256 : 2], ident[:])
-            turned[(kind, j)] = t[:].rearrange("p w k b -> p w (k b)").bitcast(BF16).rearrange("p w (b e) -> p w b e", e=2)
+                for k in range(2):
+                    for w in range(2):
+                        nc.tensor.transpose(t[:, w, k, :], words[:, k, w : 256 : 2], ident[:])
+                flat = t[:].rearrange("p w k b -> p w (k b)")
+            turned[(kind, j)] = flat.bitcast(BF16).rearrange("p w (b e) -> p w b e", e=2)
 
         def square_turn(kind, j):
             if kind == "c":
-                sq = csq[:, :, 256 * j : 256 * j + 256]
+                nc.scalar.activation(
+                    out=csq[:, :, j // 2, :, j % 2, :].rearrange("p (w e) v y -> p w e v y", e=2),
+                    in_=turned[("c", j)].rearrange("p w (v y) e -> p w e v y", v=2),
+                    func=ACT.Square,
+                )
             else:
                 sqs[j] = work.tile([P, 4, 256], F32, name="sq", tag="sq", bufs=3)
-                sq = sqs[j][:]
-            nc.scalar.activation(
-                out=sq.rearrange("p (w e) b -> p w e b", e=2),
-                in_=turned[(kind, j)].rearrange("p w b e -> p w e b"),
-                func=ACT.Square,
-            )
+                nc.scalar.activation(
+                    out=sqs[j][:].rearrange("p (w e) b -> p w e b", e=2),
+                    in_=turned[("q", j)].rearrange("p w b e -> p w e b"),
+                    func=ACT.Square,
+                )
 
         def weigh(kind, j):
             wide = g_wide if kind == "q" else h_wide
@@ -145,9 +167,20 @@ def tile_modernncastochasticneighbourregressor_kernel(tc, q, c, g, h, y_bytes, y
             prods[(kind, j)] = prod
 
         def quant(kind, j):
-            codes, scales = (q_codes, q_scales) if kind == "q" else (c_codes, c_scales)
-            cols = slice(256 * j, 256 * j + 256)
-            nc.vector.quantize_mx(out=codes[:, cols].bitcast(FP8X4), scales=scales[:, cols], in_=prods[(kind, j)][:])
+            if kind == "q":
+                cols = slice(256 * j, 256 * j + 256)
+                nc.vector.quantize_mx(
+                    out=q_codes[:, cols].bitcast(FP8X4), scales=q_scales[:, cols], in_=prods[("q", j)][:]
+                )
+            else:
+                for v in range(2):
+                    first = 512 * (j // 2) + 256 * v + 128 * (j % 2)
+                    cols = slice(first, first + 128)
+                    nc.vector.quantize_mx(
+                        out=c_codes[:, cols].bitcast(FP8X4),
+                        scales=c_scales[:, cols],
+                        in_=prods[("c", j)][:, 512 * v : 512 * v + 512],
+                    )
 
         def q2_mm(j):
             if j % 2 == 0:
@@ -178,7 +211,7 @@ def tile_modernncastochasticneighbourregressor_kernel(tc, q, c, g, h, y_bytes, y
             t = c2ps[hf]
             for s in parts:
                 nc.tensor.matmul(
-                    t[:], lhsT=gh4[:, s : s + 1].to_broadcast([P, P]), rhs=csq[:, s, cols], start=False, stop=(s == 3)
+                    t[:], lhsT=gh4[:, s : s + 1].to_broadcast([P, P]), rhs=csq[:, s, hf, :, :, :].rearrange("p v j y -> p (v j y)"), start=False, stop=(s == 3)
                 )
 
         def c2_open(hf):
@@ -247,6 +280,18 @@ def tile_modernncastochasticneighbourregressor_kernel(tc, q, c, g, h, y_bytes, y
         def y_widen(k):
             gg, t = k // 4, k % 4
             nc.scalar.activation(out=yw[:, gg, t, :], in_=yb[:, gg, t, :].bitcast(F8), func=ACT.Copy, scale=ysc[:, gg, t : t + 1])
+
+        def r_sort():
+            for gg in range(2):
+                cols = slice(512 * gg, 512 * gg + 512)
+                nc.gpsimd.tensor_scalar(
+                    out=r_wide[:, cols].rearrange("p (v x e) -> p v x e", v=2, e=2),
+                    in0=r_raw[:, cols].rearrange("p (x v e) -> p v x e", v=2, e=2),
+                    scalar1=1.0,
+                    scalar2=0.0,
+                    op0=ALU.mult,
+                    op1=ALU.add,
+                )
 
         yis = {}
 
@@ -359,6 +404,8 @@ def tile_modernncastochasticneighbourregressor_kernel(tc, q, c, g, h, y_bytes, y
                 y_widen(i + 5)
             if i == 4:
                 y_mix(1)
+            if i == 7:
+                r_sort()
             if i == 11:
                 shifts(0, 8)
         for i in range(MIN_LATE, NT):
@@ -372,7 +419,12 @@ def tile_modernncastochasticneighbourregressor_kernel(tc, q, c, g, h, y_bytes, y
         def expo(i):
             e = work.tile([P, N], F32, name="e", tag="e", bufs=3)
             nc.scalar.activation(
-                out=e[:], in_=dist[:, i, :], func=ACT.Exp, bias=shift[:, i : i + 1], scale=neg_w[:, i : i + 1], accum_out=esum[:, i : i + 1]
+                out=e[:],
+                in_=dist[:, i, :],
+                func=ACT.Exp,
+                bias=shift[:, i : i + 1],
+                scale=neg_w[:, i : i + 1],
+                accum_out=esum[:, i : i + 1],
             )
             es[i] = e
 
@@ -391,8 +443,9 @@ def tile_modernncastochasticneighbourregressor_kernel(tc, q, c, g, h, y_bytes, y
             t = psum.tile([P, len(gs), 2, P], F32, name="turn", tag="turn", bufs=3)
             words = ars[(i, gs)][:].bitcast(F32)
             for gg in range(len(gs)):
-                for w in range(2):
-                    nc.tensor.transpose(t[:, gg, w, :], words[:, 256 * gg + w : 256 * gg + 256 : 2], ident[:])
+                for v in range(2):
+                    first = 256 * gg + 128 * v
+                    nc.tensor.transpose(t[:, gg, v, :], words[:, first : first + 128], ident[:])
             ats[(i, gs)] = t
 
         def empty_ar(i, gs=(0, 1), mover=None):
@@ -429,7 +482,7 @@ def tile_modernncastochasticneighbourregressor_kernel(tc, q, c, g, h, y_bytes, y
 
         def store(i):
             o = work.tile([P, C], F32, name="o", tag="o", bufs=5)
-            if i % 2 == 1:
+            if i % 8 in (1, 4, 6):
                 nc.scalar.copy(out=o[:], in_=os_[i][:])
             else:
                 nc.vector.tensor_copy(out=o[:], in_=os_[i][:])

from contextlib import ExitStack

import concourse.mybir as mybir
from concourse.masks import make_identity

B, N, E, C = 2048, 1024, 512, 512
FLOPS = 2 * B * N * E + 2 * B * N * C

F32 = mybir.dt.float32
BF16 = mybir.dt.bfloat16
U32 = mybir.dt.uint32
U8 = mybir.dt.uint8
F8 = mybir.dt.float8_e4m3fn
FP8X4 = mybir.dt.float8_e4m3fn_x4
ALU = mybir.AluOpType
ACT = mybir.ActivationFunctionType

P = 128
HALF = 512
NT = B // P
NPAIR = NT // 2
CPAIR = N // P // 2
FAR = 2.0**58
KAPPA = 1.5
MIN_LATE = 13


def tile_modernncastochasticneighbourregressor_kernel(tc, q, c, g, h, y_bytes, y_scale, u, r, out):
    nc = tc.nc
    with ExitStack() as ctx:
        keep = ctx.enter_context(tc.tile_pool(name="keep", bufs=1))
        work = ctx.enter_context(tc.tile_pool(name="work", bufs=2))
        psum = ctx.enter_context(tc.psum_pool(name="psum", bufs=1))

        ident = keep.tile([P, P], F32, name="ident")
        ones = keep.tile([P, P], BF16, name="ones")
        sorter = keep.tile([P, P], F32, name="sorter")
        g4 = keep.tile([P, 4], BF16, name="g4")
        h4 = keep.tile([P, 4], BF16, name="h4")
        gh4 = keep.tile([P, 4], F32, name="gh4")
        g_wide = keep.tile([P, 256, 4], BF16, name="g_wide", align_bytes=64)
        h_wide = keep.tile([P, 256, 4], BF16, name="h_wide", align_bytes=64)
        u_row = keep.tile([P, N], BF16, name="u_row")
        far_row = keep.tile([P, N], BF16, name="far_row")
        r_raw = keep.tile([P, N], BF16, name="r_raw")
        r_wide = keep.tile([P, N], BF16, name="r_wide")
        c2_wide = keep.tile([P, N], F32, name="c2_wide")
        csq = keep.tile([P, 4, 2, 2, 2, P], F32, name="csq")
        c_codes = keep.tile([P, N], U32, name="c_codes", align_bytes=64)
        c_scales = keep.tile([P, N], U8, name="c_scales", align_bytes=64)
        q_codes = keep.tile([P, B], U32, name="q_codes", align_bytes=64)
        q_scales = keep.tile([P, B], U8, name="q_scales", align_bytes=64)
        ghk4 = keep.tile([P, 4], F32, name="ghk4")
        c2_low = keep.tile([P, 1], F32, name="c2_low")
        unit = keep.tile([P, NT], F32, name="unit")
        inv = keep.tile([P, NT], F32, name="inv")
        q2i = keep.tile([P, NT], F32, name="q2i")
        two_w = keep.tile([P, NT], F32, name="two_w")
        neg_w = keep.tile([P, NT], F32, name="neg_w")
        near = keep.tile([P, NT], F32, name="near")
        shift = keep.tile([P, NT], F32, name="shift")
        esum = keep.tile([P, NT], F32, name="esum")
        rsum = keep.tile([P, NT], F32, name="rsum")
        dist = keep.tile([P, NT, N], F32, name="dist")
        yb = keep.tile([P, 2, 4, C], U8, name="yb", align_bytes=64)
        ysc = keep.tile([P, 2, 4], F32, name="ysc")
        yw = keep.tile([P, 2, 4, C], BF16, name="yw", align_bytes=64)
        y_codes = keep.tile([P, 2, C], U32, name="y_codes", align_bytes=64)
        y_scales = keep.tile([P, 2, C], U8, name="y_scales", align_bytes=64)
        dummy = keep.tile([P, 1], F32, name="dummy")

        c_v = c.rearrange("(j k p) e -> j p k e", k=2, p=P)
        q_v = q.rearrange("(j k p) e -> j p k e", k=2, p=P)
        y_v = y_bytes.rearrange("(g p t) n -> p g t n", p=P, t=4)
        ysc_v = y_scale.rearrange("(g p t) o -> p g (t o)", p=P, t=4)
        out_v = out.rearrange("(i p) n -> i p n", p=P)

        ctx.enter_context(tc.manual_schedule())

        rows = {}

        def load_rows(kind, j, view):
            t = work.tile([P, 2, E], BF16, name="rows", tag="rows", bufs=12)
            nc.sync.dma_start(out=t[:], in_=view[j])
            rows[(kind, j)] = t

        nc.scalar.dma_start(out=g4[:], in_=g.rearrange("(p t) -> p t", t=4))
        nc.scalar.dma_start(out=h4[:], in_=h.rearrange("(p t) -> p t", t=4))
        nc.scalar.dma_start(out=u_row[0:1, :], in_=u.rearrange("(o n) -> o n", o=1))
        nc.scalar.dma_start(out=ysc[:], in_=ysc_v)
        load_rows("c", 0, c_v)
        load_rows("c", 1, c_v)
        load_rows("c", 2, c_v)
        load_rows("c", 3, c_v)
        load_rows("q", 0, q_v)
        load_rows("q", 1, q_v)
        nc.sync.dma_start(out=yb[:], in_=y_v)
        for j in range(2, NPAIR):
            load_rows("q", j, q_v)
        nc.sync.dma_start(out=r_raw[:], in_=r.partition_broadcast(P))

        nc.vector.memset(dummy[:], 1.0)
        nc.scalar.activation(out=dummy[:], in_=dummy[:], func=ACT.Sqrt)
        make_identity(nc, ident[:])
        nc.vector.tensor_copy(
            out=sorter[:].rearrange("p (v x e) -> p v x e", v=2, e=2), in_=ident[:].rearrange("p (x v e) -> p v x e", v=2, e=2)
        )
        nc.gpsimd.memset(far_row[:], 0.0)
        nc.gpsimd.memset(ones[:], 1.0)
        nc.vector.tensor_copy(out=g_wide[:], in_=g4[:].unsqueeze(1).to_broadcast([P, 256, 4]))
        nc.vector.tensor_copy(out=h_wide[:], in_=h4[:].unsqueeze(1).to_broadcast([P, 256, 4]))
        nc.vector.tensor_tensor(out=gh4[:], in0=g4[:], in1=h4[:], op=ALU.mult)
        nc.vector.tensor_scalar(out=ghk4[:], in0=gh4[:], scalar1=1.0 / KAPPA, scalar2=None, op0=ALU.mult)
        for gg in range(2):
            cols = slice(512 * gg, 512 * gg + 512)
            nc.vector.tensor_scalar(
                out=far_row[0:1, cols].rearrange("o (v x e) -> o v x e", v=2, e=2),
                in0=u_row[0:1, cols].rearrange("o (x v e) -> o v x e", v=2, e=2),
                scalar1=0.7,
                scalar2=FAR,
                op0=ALU.is_ge,
                op1=ALU.mult,
            )

        turned, sqs, prods, q2ps = {}, {}, {}, {}

        def turn(kind, j):
            words = rows[(kind, j)][:].bitcast(F32)
            if kind == "c":
                t = psum.tile([P, 2, 2, 2, P // 2], F32, name="bank", tag="bank", bufs=4)
                for k in range(2):
                    for w in range(2):
                        nc.tensor.transpose(t[:, w, :, k, :], words[:, k, w : 256 : 2], sorter[:])
                flat = t[:].rearrange("p w v k y -> p w (v k y)")
            else:
                t = psum.tile([P, 2, 2, P], F32, name="turn", tag="turn", bufs=3)
                for k in range(2):
                    for w in range(2):
                        nc.tensor.transpose(t[:, w, k, :], words[:, k, w : 256 : 2], ident[:])
                flat = t[:].rearrange("p w k b -> p w (k b)")
            turned[(kind, j)] = flat.bitcast(BF16).rearrange("p w (b e) -> p w b e", e=2)

        def square_turn(kind, j):
            if kind == "c":
                nc.scalar.activation(
                    out=csq[:, :, j // 2, :, j % 2, :].rearrange("p (w e) v y -> p w e v y", e=2),
                    in_=turned[("c", j)].rearrange("p w (v y) e -> p w e v y", v=2),
                    func=ACT.Square,
                )
            else:
                sqs[j] = work.tile([P, 4, 256], F32, name="sq", tag="sq", bufs=3)
                nc.scalar.activation(
                    out=sqs[j][:].rearrange("p (w e) b -> p w e b", e=2),
                    in_=turned[("q", j)].rearrange("p w b e -> p w e b"),
                    func=ACT.Square,
                )

        def weigh(kind, j):
            wide = g_wide if kind == "q" else h_wide
            prod = work.tile([P, 1024], BF16, name="prod", tag="prod", bufs=3, align_bytes=64)
            nc.vector.tensor_tensor(
                out=prod[:].rearrange("p (b w e) -> p b w e", w=2, e=2),
                in0=turned[(kind, j)].rearrange("p w b e -> p b w e"),
                in1=wide[:].rearrange("p b (w e) -> p b w e", e=2),
                op=ALU.mult,
            )
            prods[(kind, j)] = prod

        def quant(kind, j):
            if kind == "q":
                cols = slice(256 * j, 256 * j + 256)
                nc.vector.quantize_mx(
                    out=q_codes[:, cols].bitcast(FP8X4), scales=q_scales[:, cols], in_=prods[("q", j)][:]
                )
            else:
                for v in range(2):
                    first = 512 * (j // 2) + 256 * v + 128 * (j % 2)
                    cols = slice(first, first + 128)
                    nc.vector.quantize_mx(
                        out=c_codes[:, cols].bitcast(FP8X4),
                        scales=c_scales[:, cols],
                        in_=prods[("c", j)][:, 512 * v : 512 * v + 512],
                    )

        def q2_mm(j):
            if j % 2 == 0:
                q2ps[j // 2] = psum.tile([P, 4], F32, name="q2p", tag="q2p", bufs=1)
            t = q2ps[j // 2]
            for k in range(2):
                col = 2 * (j % 2) + k
                for s in range(4):
                    nc.tensor.matmul(t[:, col : col + 1], lhsT=sqs[j][:, s, P * k : P * k + P], rhs=ghk4[:, s : s + 1], start=(s == 0), stop=(s == 3))

        def q2_units(m):
            t = q2ps[m]
            cols = slice(4 * m, 4 * m + 4)
            nc.vector.tensor_scalar(out=unit[:, cols], in0=t[:], scalar1=c2_low[:], scalar2=1e-12, op0=ALU.add, op1=ALU.max)
            nc.vector.reciprocal(out=inv[:, cols], in_=unit[:, cols])
            nc.vector.scalar_tensor_tensor(out=q2i[:, cols], in0=t[:], scalar=KAPPA, in1=inv[:, cols], op0=ALU.mult, op1=ALU.mult)

        def q2_w(m):
            cols = slice(4 * m, 4 * m + 4)
            nc.scalar.activation(out=two_w[:, cols], in_=unit[:, cols], func=ACT.Sqrt, scale=4.0)

        c2ps = {}

        def c2_mm(hf, parts=(0, 1, 2, 3)):
            cols = slice(HALF * hf, HALF * hf + HALF)
            if parts[0] == 0:
                c2_open(hf)
            t = c2ps[hf]
            for s in parts:
                nc.tensor.matmul(
                    t[:], lhsT=gh4[:, s : s + 1].to_broadcast([P, P]), rhs=csq[:, s, hf, :, :, :].rearrange("p v j y -> p (v j y)"), start=False, stop=(s == 3)
                )

        def c2_open(hf):
            t = psum.tile([P, HALF], F32, name="turn", tag="turn", bufs=3)
            c2ps[hf] = t
            cols = slice(HALF * hf, HALF * hf + HALF)
            nc.tensor.matmul(t[:], lhsT=ones[:], rhs=far_row[:, cols], start=True, stop=False)

        def c2_copy(hf):
            cols = slice(HALF * hf, HALF * hf + HALF)
            nc.scalar.copy(out=c2_wide[:, cols], in_=c2ps[hf][:])

        def c2_low_calc():
            if True:
                nc.vector.tensor_reduce(out=c2_low[:], in_=c2_wide[:, :P], axis=mybir.AxisListType.X, op=ALU.min)
                nc.vector.tensor_scalar(out=c2_low[:], in0=c2_low[:], scalar1=1.0 / KAPPA, scalar2=None, op0=ALU.mult)

        crosses, ss = {}, {}

        def cross(i, hfs=(0, 1)):
            for hf in hfs:
                t = psum.tile([P, HALF], F32, name="bank", tag="bank", bufs=4)
                b_cols = slice(P * i, P * i + P)
                n_cols = slice(HALF * hf, HALF * hf + HALF)
                nc.tensor.matmul_mx(
                    out=t[:],
                    lhsT=q_codes[:, b_cols].bitcast(FP8X4),
                    lhsT_scale=q_scales[:, b_cols],
                    rhs=c_codes[:, n_cols].bitcast(FP8X4),
                    rhs_scale=c_scales[:, n_cols],
                    start=True,
                    stop=True,
                )
                crosses[(i, hf)] = t

        def add_c2(i, hfs=(0, 1)):
            s = dist[:, i, :]
            for hf in hfs:
                n_cols = slice(HALF * hf, HALF * hf + HALF)
                nc.vector.scalar_tensor_tensor(
                    out=s[:, n_cols], in0=crosses[(i, hf)][:], scalar=-2.0, in1=c2_wide[:, n_cols], op0=ALU.mult, op1=ALU.add
                )
            ss[i] = s

        lows = {}

        def narrow(i):
            low = work.tile([P, N], BF16, name="low", tag="low", bufs=3)
            nc.gpsimd.tensor_scalar(out=low[:], in0=dist[:, i, :], scalar1=1.0, scalar2=0.0, op0=ALU.mult, op1=ALU.add)
            lows[i] = low

        def row_min(i):
            junk = work.tile([P, N], BF16, name="junk", tag="junk", bufs=1)
            nc.vector.tensor_scalar(
                out=junk[:], in0=lows[i][:], scalar1=1.0, scalar2=None, op0=ALU.mult, op1=ALU.min, accum_out=near[:, i : i + 1]
            )

        def root(i):
            nc.scalar.activation(out=dist[:, i, :], in_=ss[i], func=ACT.Sqrt, bias=q2i[:, i : i + 1], scale=inv[:, i : i + 1])

        def shifts(i0, i1):
            cols = slice(i0, i1)
            nc.vector.tensor_scalar(out=neg_w[:, cols], in0=two_w[:, cols], scalar1=-1.0, scalar2=None, op0=ALU.mult)
            nc.vector.tensor_tensor(out=shift[:, cols], in0=two_w[:, cols], in1=near[:, cols], op=ALU.mult)

        def y_widen(k):
            gg, t = k // 4, k % 4
            nc.scalar.activation(out=yw[:, gg, t, :], in_=yb[:, gg, t, :].bitcast(F8), func=ACT.Copy, scale=ysc[:, gg, t : t + 1])

        def r_sort():
            for gg in range(2):
                cols = slice(512 * gg, 512 * gg + 512)
                nc.gpsimd.tensor_scalar(
                    out=r_wide[:, cols].rearrange("p (v x e) -> p v x e", v=2, e=2),
                    in0=r_raw[:, cols].rearrange("p (x v e) -> p v x e", v=2, e=2),
                    scalar1=1.0,
                    scalar2=0.0,
                    op0=ALU.mult,
                    op1=ALU.add,
                )

        yis = {}

        def y_mix(gg):
            yi = work.tile([P, C, 4], BF16, name="yi", tag="yi", bufs=2, align_bytes=64)
            nc.gpsimd.tensor_scalar(
                out=yi[:], in0=yw[:, gg, :, :].rearrange("p t n -> p n t"), scalar1=1.0, scalar2=0.0, op0=ALU.mult, op1=ALU.add
            )
            yis[gg] = yi

        def y_quant(gg):
            nc.vector.quantize_mx(
                out=y_codes[:, gg, :].bitcast(FP8X4), scales=y_scales[:, gg, :], in_=yis[gg][:].rearrange("p n t -> p (n t)")
            )

        for j in range(4):
            turn("c", j)
            square_turn("c", j)
            weigh("c", j)
            if j > 1:
                quant("c", j - 2)
        turn("q", 0)
        turn("q", 1)
        c2_mm(0)
        weigh("q", 0)
        quant("c", 2)
        weigh("q", 1)
        quant("c", 3)
        square_turn("q", 0)
        quant("q", 0)
        y_widen(0)
        quant("q", 1)
        cross(0, (0,))
        cross(1, (0,))
        c2_copy(0)
        square_turn("q", 1)
        turn("q", 2)
        cross(2, (0,))
        c2_mm(1, (0,))
        cross(3, (0,))
        y_widen(1)
        add_c2(0, (0,))
        add_c2(1, (0,))
        weigh("q", 2)
        square_turn("q", 2)
        add_c2(2, (0,))
        turn("q", 3)
        quant("q", 2)
        add_c2(3, (0,))
        c2_mm(1, (1,))
        cross(4, (0,))
        y_widen(2)
        y_widen(3)
        y_mix(0)
        c2_mm(1, (2,))
        c2_low_calc()
        cross(5, (0,))
        weigh("q", 3)
        add_c2(4, (0,))
        q2_mm(0)
        quant("q", 3)
        add_c2(5, (0,))
        c2_mm(1, (3,))
        cross(6, (0,))
        add_c2(6, (0,))
        c2_copy(1)
        cross(0, (1,))
        q2_mm(1)
        cross(1, (1,))
        cross(7, (0,))
        add_c2(0, (1,))
        y_widen(4)
        q2_units(0)
        square_turn("q", 3)
        add_c2(7, (0,))
        cross(2, (1,))
        add_c2(1, (1,))
        for i in range(NT):
            even, j = i % 2 == 0, i // 2
            live = lambda p: 4 <= p < NPAIR
            if i + 3 < 8:
                cross(i + 3, (1,))
            elif i + 3 < NT:
                cross(i + 3)
            if even and live(j + 4):
                turn("q", j + 4)
            root(i)
            narrow(i)
            if i + 2 < 8:
                add_c2(i + 2, (1,))
            elif i + 2 < NT:
                add_c2(i + 2)
            if not even and live(j + 4):
                weigh("q", j + 4)
                square_turn("q", j + 4)
            if 0 <= i - 2 < MIN_LATE:
                row_min(i - 2)
            if i % 4 == 1 and i + 3 < NT:
                q2_units((i + 3) // 4)
            if even and live(j + 3):
                quant("q", j + 3)
            if i == 0:
                q2_mm(2)
                q2_mm(3)
            if even and live(j + 3):
                q2_mm(j + 3)
            if i % 4 == 0:
                q2_w(i // 4)
            if i < 3:
                y_widen(i + 5)
            if i == 4:
                y_mix(1)
            if i == 7:
                r_sort()
            if i == 11:
                shifts(0, 8)
        for i in range(MIN_LATE, NT):
            row_min(i)
        y_quant(0)
        y_quant(1)
        shifts(8, 16)

        es, ars, ats, ins, acs, os_ = {}, {}, {}, {}, {}, {}

        def expo(i):
            e = work.tile([P, N], F32, name="e", tag="e", bufs=3)
            nc.scalar.activation(
                out=e[:],
                in_=dist[:, i, :],
                func=ACT.Exp,
                bias=shift[:, i : i + 1],
                scale=neg_w[:, i : i + 1],
                accum_out=esum[:, i : i + 1],
            )
            es[i] = e

        def invert(i):
            nc.vector.reciprocal(out=rsum[:, i : i + 1], in_=esum[:, i : i + 1])

        def scale_ar(i, gs=(0, 1)):
            cols = slice(512 * gs[0], 512 * gs[-1] + 512)
            ar = work.tile([P, 512 * len(gs)], BF16, name="ar", tag="ar", bufs=3, align_bytes=64)
            nc.vector.scalar_tensor_tensor(
                out=ar[:], in0=es[i][:, cols], scalar=rsum[:, i : i + 1], in1=r_wide[:, cols], op0=ALU.mult, op1=ALU.mult
            )
            ars[(i, gs)] = ar

        def turn_ar(i, gs=(0, 1)):
            t = psum.tile([P, len(gs), 2, P], F32, name="turn", tag="turn", bufs=3)
            words = ars[(i, gs)][:].bitcast(F32)
            for gg in range(len(gs)):
                for v in range(2):
                    first = 256 * gg + 128 * v
                    nc.tensor.transpose(t[:, gg, v, :], words[:, first : first + 128], ident[:])
            ats[(i, gs)] = t

        def empty_ar(i, gs=(0, 1), mover=None):
            mover = mover or nc.scalar.copy
            a_in = work.tile([P, len(gs), P, 4], BF16, name="a_in", tag="a_in", bufs=3, align_bytes=64)
            mover(out=a_in[:].bitcast(F32), in_=ats[(i, gs)][:].rearrange("p g w b -> p g b w"))
            ins[(i, gs)] = a_in

        def quant_ar(i, gs=(0, 1)):
            codes = work.tile([P, len(gs), P], U32, name="a_codes", tag="a_codes", bufs=3, align_bytes=64)
            scales = work.tile([P, len(gs), P], U8, name="a_scales", tag="a_scales", bufs=3, align_bytes=64)
            nc.vector.quantize_mx(
                out=codes[:].rearrange("p g b -> p (g b)").bitcast(FP8X4),
                scales=scales[:].rearrange("p g b -> p (g b)"),
                in_=ins[(i, gs)][:].rearrange("p g b t -> p (g b t)"),
            )
            for n, gg in enumerate(gs):
                acs[(i, gg)] = codes[:, n, :], scales[:, n, :]

        def mm_out(i, gs=(0, 1)):
            if gs[0] == 0:
                os_[i] = psum.tile([P, HALF], F32, name="bank", tag="bank", bufs=4)
            for gg in gs:
                codes, scales = acs[(i, gg)]
                nc.tensor.matmul_mx(
                    out=os_[i][:],
                    lhsT=codes.bitcast(FP8X4),
                    lhsT_scale=scales,
                    rhs=y_codes[:, gg, :].bitcast(FP8X4),
                    rhs_scale=y_scales[:, gg, :],
                    start=(gg == 0),
                    stop=(gg == 1),
                )

        def store(i):
            o = work.tile([P, C], F32, name="o", tag="o", bufs=5)
            if i % 8 in (1, 4, 6):
                nc.scalar.copy(out=o[:], in_=os_[i][:])
            else:
                nc.vector.tensor_copy(out=o[:], in_=os_[i][:])
            nc.sync.dma_start(out=out_v[i], in_=o[:])

        def store_halves(i):
            for cc, mover in ((0, nc.scalar.copy), (1, nc.vector.tensor_copy)):
                o = work.tile([P, C // 2], F32, name="o", tag="o", bufs=5)
                cols = slice(256 * cc, 256 * cc + 256)
                mover(out=o[:], in_=os_[i][:, cols])
                nc.sync.dma_start(out=out_v[i][:, cols], in_=o[:])

        last = NT - 1
        for k in range(NT + 2):
            if k < NT:
                expo(k)
            if 0 <= k - 1 < last:
                scale_ar(k - 1)
                turn_ar(k - 1)
            if k - 1 == last:
                scale_ar(last, (0,))
                turn_ar(last, (0,))
                scale_ar(last, (1,))
                turn_ar(last, (1,))
            if 0 <= k - 2 < last:
                empty_ar(k - 2)
            if 0 <= k - 3 < last:
                quant_ar(k - 3)
                mm_out(k - 3)
            if k < NT:
                invert(k)
            if 0 <= k - 4 < last:
                store(k - 4)
        empty_ar(last, (0,))
        quant_ar(last, (0,))
        mm_out(last, (0,))
        empty_ar(last, (1,), nc.vector.tensor_copy)
        quant_ar(last, (1,))
        mm_out(last, (1,))
        store(last - 1)
        store_halves(last)
